import numpy as np
import ml_dtypes


def mxq(x, axis, fmt="e4m3"):
    dtype, down = {"e4m3": (ml_dtypes.float8_e4m3fn, 7), "e5m2": (ml_dtypes.float8_e5m2, 14)}[fmt]
    v = np.moveaxis(np.asarray(x, np.float32).astype(ml_dtypes.bfloat16).astype(np.float64), axis, -1)
    blocks = v.reshape(v.shape[:-1] + (-1, 32))
    amax = np.abs(blocks).max(-1, keepdims=True)
    byte = np.maximum(np.where(amax > 0, np.frexp(amax)[1] - 1 + 127, 0) - down, 1)
    scale = np.exp2(byte - 127.0)
    codes = (blocks / scale).astype(np.float32).astype(dtype).astype(np.float64)
    return np.moveaxis((codes * scale).reshape(v.shape), -1, axis)


WIDE = False


def mx_kscale(k):
    if not WIDE:
        return np.ones(k)
    levels = np.array([30, -30])
    if k % 512:
        return np.exp2(np.random.permutation(np.resize(levels, k // 32))).repeat(32)
    a = np.empty((k // 512, 16))
    for p in range(k // 512):
        a[p, :8] = np.random.permutation(np.resize(levels, 8))
        for g in range(8):
            far = levels[np.abs(levels - a[p, g]) >= 10]
            a[p, g + 8] = far[np.random.randint(len(far))]
    return np.exp2(a.ravel()).repeat(32)


def f64(x):
    return np.asarray(x).astype(np.float64)


def striped(idx):
    return np.tile(np.asarray(idx).reshape(-1, 16).T, (8, 1)).astype(np.uint16)


def unstriped(offs):
    return offs[:16].T.reshape(-1).astype(np.int64)


def striped8(idx):
    return np.asarray(idx).reshape(8, -1, 16).transpose(0, 2, 1).reshape(128, -1).astype(np.uint16)


def unstriped8(offs):
    return offs.reshape(8, 16, -1).transpose(0, 2, 1).reshape(8, -1).astype(np.int64)


def pick8(x, idx, run):
    r = np.arange(len(x))
    return x[r[:, None], idx[r % (8 * run) // run]]


E2M1 = np.array([0.0, 0.5, 1.0, 1.5, 2.0, 3.0, 4.0, 6.0, -0.0, -0.5, -1.0, -1.5, -2.0, -3.0, -4.0, -6.0])


def pack_weight(w, fmt):
    k, n = w.shape
    w = f64(np.asarray(w, np.float32).astype(ml_dtypes.bfloat16)).reshape(k // 32, 32, n)
    amax = np.abs(w).max(1)
    if fmt in ("e4m3", "e5m2"):
        byte = np.frexp(amax)[1] - 1 + 127 - (7 if fmt == "e4m3" else 14)
    else:
        mant, ex = np.frexp(amax / 6.0)
        byte = np.where(mant > 0.5, ex, ex - 1) + 127
    byte = np.clip(np.where(amax > 0, byte, 1), 1, 254)
    scaled = (w * np.exp2(127.0 - byte)[:, None, :]).reshape(k, n).astype(np.float32)
    by_word = np.ascontiguousarray(scaled.reshape(k // 512, 128, 4, n).transpose(0, 1, 3, 2))
    if fmt in ("e4m3", "e5m2"):
        words = by_word.astype(ml_dtypes.float8_e4m3fn if fmt == "e4m3" else ml_dtypes.float8_e5m2).view(np.uint8)
    else:
        c = by_word.astype(ml_dtypes.float4_e2m1fn).view(np.uint8) & 0xF
        words = (c[..., 0::2] | (c[..., 1::2] << 4)).reshape(k // 512, 128, 2 * n)
    return np.ascontiguousarray(words), np.ascontiguousarray(byte.astype(np.uint8).reshape(k // 512, 16, n))


def unpack_weight(words, scales, fmt):
    g, _, n = scales.shape
    words = np.ascontiguousarray(words).reshape(g, 128, n, -1)
    if fmt in ("e4m3", "e5m2"):
        vals = words.view(ml_dtypes.float8_e4m3fn if fmt == "e4m3" else ml_dtypes.float8_e5m2).astype(np.float64)
    else:
        nib = np.empty((g, 128, n, 4), np.uint8)
        nib[..., 0::2] = words & 0xF
        nib[..., 1::2] = words >> 4
        vals = E2M1[nib]
    vals = vals * np.repeat(np.exp2(scales.astype(np.float64) - 127.0), 8, axis=1)[..., None]
    return vals.transpose(0, 1, 3, 2).reshape(g * 512, n)


K, T, J, R, V, C, O, N, S = 512, 1024, 256, 512, 1024, 512, 128, 256, 1024


def setup_inputs():
    n = np.random.standard_normal
    idx = np.random.permutation(V)[:R]
    idx2 = np.random.permutation(T)[:J]
    idx3 = np.stack([np.random.permutation(C)[:J] for _ in range(8)])
    idx4 = np.random.permutation(C)[:O]
    idx5 = np.random.permutation(J)[:O]
    idx6 = np.random.permutation(S)[:N]
    fk = mx_kscale(K)
    fr = mx_kscale(R)
    tr = np.ones(V)
    tr[idx] = fr
    xtp = pack_weight(n((K, T)) / fk[:, None], "e2m1")
    wtp = pack_weight(n((K, V)) * 1 / np.sqrt(K) * fk[:, None] * tr, "e5m2")
    w2p = pack_weight(n((K, R)) * 1 / np.sqrt(K) * fk[:, None], "e4m3")
    vsp = pack_weight(n((R, S)) * 1 / np.sqrt(R) / fr[:, None], "e4m3")
    return {
        "xt_words": xtp[0],
        "xt_scales": xtp[1],
        "wt_words": wtp[0],
        "wt_scales": wtp[1],
        "w2_words": w2p[0],
        "w2_scales": w2p[1],
        "vs_words": vsp[0],
        "vs_scales": vsp[1],
        "offs": striped(idx),
        "offs2": striped(idx2),
        "offs3": striped8(idx3),
        "offs4": striped(idx4),
        "offs5": striped(idx5),
        "offs6": striped(idx6),
    }


def reference(xt_words, xt_scales, wt_words, wt_scales, w2_words, w2_scales, vs_words, vs_scales, offs, offs2, offs3, offs4, offs5, offs6):
    idx = unstriped(offs)
    idx2 = unstriped(offs2)
    idx3 = unstriped8(offs3)
    idx4 = unstriped(offs4)
    idx5 = unstriped(offs5)
    idx6 = unstriped(offs6)
    xtu = unpack_weight(xt_words, xt_scales, "e2m1")
    wtu = unpack_weight(wt_words, wt_scales, "e5m2")
    w2u = unpack_weight(w2_words, w2_scales, "e4m3")
    vsu = unpack_weight(vs_words, vs_scales, "e4m3")
    wtidxg = wtu[:, idx]
    xtidx2g = xtu[:, idx2]
    a = wtidxg.T @ xtidx2g
    b = w2u.T @ xtidx2g
    lb = b[:, 0:1]
    la = a[:, 0:1]
    pw = np.zeros((R, C))
    pw[np.arange(R)[:, None], idx3[np.arange(R) % 512 // 64]] = a
    hid = np.maximum(pw[:, idx4] * lb, b[:, idx5] * la)
    vsidx6g = vsu[:, idx6]
    hidq = mxq(hid, 0, "e5m2")
    y = vsidx6g.T @ hidq
    return y

@@ -1,0 +1,150 @@
+from contextlib import ExitStack
+
+import concourse.mybir as mybir
+
+F32 = mybir.dt.float32
+BF16 = mybir.dt.bfloat16
+I32 = mybir.dt.int32
+U32 = mybir.dt.uint32
+U16 = mybir.dt.uint16
+U8 = mybir.dt.uint8
+E4M3 = mybir.dt.float8_e4m3fn_x4
+E5M2 = mybir.dt.float8_e5m2_x4
+E2M1 = mybir.dt.float4_e2m1fn_x4
+COPY = mybir.ActivationFunctionType.Copy
+MAX = mybir.AluOpType.max
+
+K, T, J, R, V, C, O, N, S = 512, 1024, 256, 512, 1024, 512, 128, 256, 1024
+P = 128
+PACK = 4
+FLOPS = 2 * K * R * J * 2 + 2 * R * N * O
+
+
+def tile_list_ownlead_storeleads_store_plain_kernel(tc, xt_words, xt_scales, wt_words, wt_scales, w2_words, w2_scales, vs_words, vs_scales, offs, offs2, offs3, offs4, offs5, offs6, out):
+    nc = tc.nc
+    with ExitStack() as ctx:
+        sb = ctx.enter_context(tc.tile_pool(name="sb", bufs=1))
+        ps = ctx.enter_context(tc.psum_pool(name="ps", bufs=1))
+
+        def new(name, cols, dtype):
+            return sb.tile([P, cols], dtype, name=name, align_bytes=64)
+
+        def load_list(name, src):
+            tile = sb.tile(list(src.shape), U16, name=name)
+            nc.sync.dma_start(tile[:], src)
+            return tile
+
+        def load_words(eng, tile, src):
+            eng.dma_start(out=tile[:].bitcast(I32), in_=src.bitcast(I32))
+
+        def load_scales(eng, tile, src):
+            for q in range(4):
+                eng.dma_start(out=tile[32 * q : 32 * q + 4, :].bitcast(I32), in_=src[0, 4 * q : 4 * q + 4, :].bitcast(I32))
+
+        def load_scales_whole(tile, src):
+            for q in range(4):
+                nc.sync.dma_start(out=tile[32 * q : 32 * q + 32, :].bitcast(I32), in_=src[0, 4 * q : 4 * q + 4, :].bitcast(I32).partition_broadcast(8))
+
+        xs, ws, w2s, vss = new("xs", T, U8), new("ws", V, U8), new("w2s", R, U8), new("vss", S, U8)
+        xw, ww, w2w, vsw = new("xw", T, U16), new("ww", V, U32), new("w2w", R, U32), new("vsw", S, U32)
+        for tile in (w2s, vss):
+            nc.vector.memset(tile[:].bitcast(I32), 0)
+        pw = [new("pw%d" % t, C, F32) for t in range(PACK)]
+        for t in range(PACK):
+            nc.vector.memset(pw[t][:], 0.0)
+
+        merge = "p n t -> p (n t)"
+        load_words(nc.scalar, xw, xt_words[0])
+        o2 = load_list("o2", offs2)
+        load_words(nc.scalar, ww, wt_words[0].rearrange(merge))
+        o1 = load_list("o1", offs)
+        load_scales_whole(ws, wt_scales)
+        load_scales_whole(xs, xt_scales)
+        o3 = load_list("o3", offs3)
+        load_words(nc.sync, w2w, w2_words[0].rearrange(merge))
+        load_scales(nc.sync, w2s, w2_scales)
+        o4 = load_list("o4", offs4)
+        o5 = load_list("o5", offs5)
+        o6 = load_list("o6", offs6)
+        load_words(nc.sync, vsw, vs_words[0].rearrange(merge))
+        load_scales(nc.sync, vss, vs_scales)
+
+        xwg, xsg = new("xwg", J, U16), new("xsg", J, U8)
+        wwg, wsg = new("wwg", R, U32), new("wsg", R, U8)
+        nc.vector.tensor_copy(xwg[:], xw[:].indirect(o2[:]))
+        nc.vector.tensor_copy(wsg[:], ws[:].indirect(o1[:]))
+        nc.vector.tensor_copy(wwg[:], ww[:].indirect(o1[:]))
+
+        def dealt(tile):
+            return tile.rearrange("p (m t) -> p t m", t=PACK)
+
+        def regrouped(tile, count):
+            return tile.rearrange("p (t m) -> p t m", t=count)
+
+        ww0, ws0 = new("ww0", P, U32), new("ws0", P, U8)
+        ww3, ws3 = new("ww3", 3 * P, U32), new("ws3", 3 * P, U8)
+        nc.vector.tensor_copy(ws0[:], dealt(wsg[:])[:, 0, :])
+        nc.vector.tensor_copy(ww0[:].bitcast(I32), dealt(wwg[:].bitcast(I32))[:, 0, :])
+
+        nc.vector.tensor_copy(xsg[:], xs[:].indirect(o2[:]))
+        a_ps = [ps.tile([P, J], F32, name="a_ps%d" % t) for t in range(PACK)]
+        b_ps = [ps.tile([P, 2, J], F32, name="b_ps%d" % h) for h in range(2)]
+        a = [new("a%d" % t, J, F32) for t in range(PACK)]
+        b = [new("b%d" % t, J, F32) for t in range(PACK)]
+
+        def first_product(dst, words, scales, fmt):
+            nc.tensor.matmul_mx(out=dst, lhsT=words.bitcast(fmt), lhsT_scale=scales, rhs=xwg[:].bitcast(E2M1), rhs_scale=xsg[:], start=True, stop=True)
+
+        first_product(a_ps[0][:], ww0[:], ws0[:], E5M2)
+        nc.scalar.copy(a[0][:], a_ps[0][:])
+        nc.scalar.activation(out=pw[0][:].indirect(o3[:]), in_=a[0][:], func=COPY)
+
+        nc.vector.tensor_copy(regrouped(ww3[:].bitcast(I32), 3), dealt(wwg[:].bitcast(I32))[:, 1:4, :])
+        nc.vector.tensor_copy(regrouped(ws3[:], 3), dealt(wsg[:])[:, 1:4, :])
+        for t in range(1, PACK):
+            cols = slice((t - 1) * P, t * P)
+            first_product(a_ps[t][:], ww3[:, cols], ws3[:, cols], E5M2)
+            nc.vector.tensor_copy(a[t][:], a_ps[t][:])
+            nc.scalar.activation(out=pw[t][:].indirect(o3[:]), in_=a[t][:], func=COPY)
+
+        w2wd, w2sd = new("w2wd", R, U32), new("w2sd", R, U8)
+        nc.vector.tensor_copy(regrouped(w2wd[:].bitcast(I32), PACK), dealt(w2w[:].bitcast(I32)))
+        nc.vector.tensor_copy(regrouped(w2sd[:], PACK), dealt(w2s[:]))
+        for t in range(PACK):
+            cols = slice(t * P, (t + 1) * P)
+            first_product(b_ps[t // 2][:, t % 2, :], w2wd[:, cols], w2sd[:, cols], E4M3)
+        for t in range(PACK):
+            nc.vector.tensor_copy(b[t][:], b_ps[t // 2][:, t % 2, :])
+
+        vwg, vsg = new("vwg", N, U32), new("vsg", N, U8)
+        nc.vector.tensor_copy(vwg[:], vsw[:].indirect(o6[:]))
+        nc.vector.tensor_copy(vsg[:], vss[:].indirect(o6[:]))
+
+        gp, gb = new("gp", PACK * O, F32), new("gb", PACK * O, F32)
+        for t in range(PACK):
+            cols = slice(t * O, (t + 1) * O)
+            nc.scalar.activation(out=gb[:, cols], in_=b[t][:].indirect(o5[:]), func=COPY, scale=a[t][:, 0:1])
+            nc.scalar.activation(out=gp[:, cols], in_=pw[t][:].indirect(o4[:]), func=COPY, scale=b[t][:, 0:1])
+
+        hid = new("hid", O * PACK, BF16)
+        by_slot = "p (t c i) -> p c t i"
+        nc.vector.tensor_tensor(
+            out=hid[:].rearrange("p (c i t) -> p c t i", i=4, t=PACK),
+            in0=gp[:].rearrange(by_slot, t=PACK, i=4),
+            in1=gb[:].rearrange(by_slot, t=PACK, i=4),
+            op=MAX,
+        )
+        hw, hs = new("hw", O, U32), new("hs", O, U8)
+        nc.vector.quantize_mx(out=hw[:].bitcast(E5M2), scales=hs[:], in_=hid[:])
+
+        for h in range(2):
+            cols = slice(h * P, (h + 1) * P)
+            y_ps = ps.tile([P, O], F32, name="y_ps%d" % h)
+            y = new("y%d" % h, O, F32)
+            nc.tensor.matmul_mx(out=y_ps[:], lhsT=vwg[:, cols].bitcast(E4M3), lhsT_scale=vsg[:, cols], rhs=hw[:].bitcast(E5M2), rhs_scale=hs[:], start=True, stop=True)
+            if h == 0:
+                nc.vector.tensor_copy(y[:], y_ps[:])
+                nc.sync.dma_start(out=out[cols, :], in_=y[:])
+            else:
+                nc.scalar.copy(y[:], y_ps[:])
+                nc.scalar.dma_start(out=out[cols, :], in_=y[:])

@@ -24,6 +24,7 @@ def tile_list_ownlead_storeleads_store_plain_kernel(tc, xt_words, xt_scales, wt_
     nc = tc.nc
     with ExitStack() as ctx:
         sb = ctx.enter_context(tc.tile_pool(name="sb", bufs=1))
+        shared = ctx.enter_context(tc.tile_pool(name="shared", bufs=1))
         ps = ctx.enter_context(tc.psum_pool(name="ps", bufs=1))
 
         def new(name, cols, dtype):
@@ -41,11 +42,11 @@ def tile_list_ownlead_storeleads_store_plain_kernel(tc, xt_words, xt_scales, wt_
             for q in range(4):
                 eng.dma_start(out=tile[32 * q : 32 * q + 4, :].bitcast(I32), in_=src[0, 4 * q : 4 * q + 4, :].bitcast(I32))
 
-        def load_scales_whole(tile, src):
+        def load_scales_whole(engs, tile, src):
             for q in range(4):
-                nc.sync.dma_start(out=tile[32 * q : 32 * q + 32, :].bitcast(I32), in_=src[0, 4 * q : 4 * q + 4, :].bitcast(I32).partition_broadcast(8))
+                engs[q].dma_start(out=tile[32 * q : 32 * q + 32, :].bitcast(I32), in_=src[0, 4 * q : 4 * q + 4, :].bitcast(I32).partition_broadcast(8))
 
-        xs, ws, w2s, vss = new("xs", T, U8), new("ws", V, U8), new("w2s", R, U8), new("vss", S, U8)
+        xs, ws, w2s, vss = shared.tile([P, T], U8, name="xs", align_bytes=64, offset=0), new("ws", V, U8), new("w2s", R, U8), new("vss", S, U8)
         xw, ww, w2w, vsw = new("xw", T, U16), new("ww", V, U32), new("w2w", R, U32), new("vsw", S, U32)
         for tile in (w2s, vss):
             nc.vector.memset(tile[:].bitcast(I32), 0)
@@ -54,13 +55,13 @@ def tile_list_ownlead_storeleads_store_plain_kernel(tc, xt_words, xt_scales, wt_
             nc.vector.memset(pw[t][:], 0.0)
 
         merge = "p n t -> p (n t)"
-        load_words(nc.scalar, xw, xt_words[0])
-        o2 = load_list("o2", offs2)
-        load_words(nc.scalar, ww, wt_words[0].rearrange(merge))
         o1 = load_list("o1", offs)
-        load_scales_whole(ws, wt_scales)
-        load_scales_whole(xs, xt_scales)
+        load_scales_whole([nc.scalar, nc.sync, nc.scalar, nc.sync], ws, wt_scales)
+        o2 = load_list("o2", offs2)
+        load_words(nc.scalar, xw, xt_words[0])
+        load_words(nc.sync, ww, wt_words[0].rearrange(merge))
         o3 = load_list("o3", offs3)
+        load_scales_whole([nc.sync] * 4, xs, xt_scales)
         load_words(nc.sync, w2w, w2_words[0].rearrange(merge))
         load_scales(nc.sync, w2s, w2_scales)
         o4 = load_list("o4", offs4)
@@ -71,21 +72,17 @@ def tile_list_ownlead_storeleads_store_plain_kernel(tc, xt_words, xt_scales, wt_
 
         xwg, xsg = new("xwg", J, U16), new("xsg", J, U8)
         wwg, wsg = new("wwg", R, U32), new("wsg", R, U8)
-        nc.vector.tensor_copy(xwg[:], xw[:].indirect(o2[:]))
         nc.vector.tensor_copy(wsg[:], ws[:].indirect(o1[:]))
+        nc.vector.tensor_copy(xwg[:], xw[:].indirect(o2[:]))
         nc.vector.tensor_copy(wwg[:], ww[:].indirect(o1[:]))
 
-        def dealt(tile):
-            return tile.rearrange("p (m t) -> p t m", t=PACK)
-
-        def regrouped(tile, count):
-            return tile.rearrange("p (t m) -> p t m", t=count)
+        def deal(dst, src, lo, hi):
+            nc.vector.tensor_copy(dst.rearrange("p (t m) -> p m t", t=hi - lo), src.rearrange("p (m t) -> p m t", t=PACK)[:, :, lo:hi])
 
         ww0, ws0 = new("ww0", P, U32), new("ws0", P, U8)
-        ww3, ws3 = new("ww3", 3 * P, U32), new("ws3", 3 * P, U8)
-        nc.vector.tensor_copy(ws0[:], dealt(wsg[:])[:, 0, :])
-        nc.vector.tensor_copy(ww0[:].bitcast(I32), dealt(wwg[:].bitcast(I32))[:, 0, :])
-
+        ww3, ws3 = shared.tile([P, 3 * P], U32, name="ww3", align_bytes=64, offset=640), shared.tile([P, 3 * P], U8, name="ws3", align_bytes=64, offset=256)
+        deal(ws0[:], wsg[:], 0, 1)
+        deal(ww0[:].bitcast(I32), wwg[:].bitcast(I32), 0, 1)
         nc.vector.tensor_copy(xsg[:], xs[:].indirect(o2[:]))
         a_ps = [ps.tile([P, J], F32, name="a_ps%d" % t) for t in range(PACK)]
         b_ps = [ps.tile([P, 2, J], F32, name="b_ps%d" % h) for h in range(2)]
@@ -98,42 +95,33 @@ def tile_list_ownlead_storeleads_store_plain_kernel(tc, xt_words, xt_scales, wt_
         first_product(a_ps[0][:], ww0[:], ws0[:], E5M2)
         nc.scalar.copy(a[0][:], a_ps[0][:])
         nc.scalar.activation(out=pw[0][:].indirect(o3[:]), in_=a[0][:], func=COPY)
-
-        nc.vector.tensor_copy(regrouped(ww3[:].bitcast(I32), 3), dealt(wwg[:].bitcast(I32))[:, 1:4, :])
-        nc.vector.tensor_copy(regrouped(ws3[:], 3), dealt(wsg[:])[:, 1:4, :])
+        deal(ws3[:], wsg[:], 1, PACK)
+        deal(ww3[:].bitcast(I32), wwg[:].bitcast(I32), 1, PACK)
         for t in range(1, PACK):
             cols = slice((t - 1) * P, t * P)
             first_product(a_ps[t][:], ww3[:, cols], ws3[:, cols], E5M2)
             nc.vector.tensor_copy(a[t][:], a_ps[t][:])
             nc.scalar.activation(out=pw[t][:].indirect(o3[:]), in_=a[t][:], func=COPY)
 
-        w2wd, w2sd = new("w2wd", R, U32), new("w2sd", R, U8)
-        nc.vector.tensor_copy(regrouped(w2wd[:].bitcast(I32), PACK), dealt(w2w[:].bitcast(I32)))
-        nc.vector.tensor_copy(regrouped(w2sd[:], PACK), dealt(w2s[:]))
+        w2wd, w2sd = shared.tile([P, R], U32, name="w2wd", align_bytes=64, offset=1152), shared.tile([P, R], U8, name="w2sd", align_bytes=64, offset=640)
+        deal(w2sd[:], w2s[:], 0, PACK)
+        deal(w2wd[:].bitcast(I32), w2w[:].bitcast(I32), 0, PACK)
         for t in range(PACK):
             cols = slice(t * P, (t + 1) * P)
             first_product(b_ps[t // 2][:, t % 2, :], w2wd[:, cols], w2sd[:, cols], E4M3)
         for t in range(PACK):
             nc.vector.tensor_copy(b[t][:], b_ps[t // 2][:, t % 2, :])
 
-        vwg, vsg = new("vwg", N, U32), new("vsg", N, U8)
+        vwg, vsg = shared.tile([P, N], U32, name="vwg", align_bytes=64, offset=1408), shared.tile([P, N], U8, name="vsg", align_bytes=64, offset=1152)
         nc.vector.tensor_copy(vwg[:], vsw[:].indirect(o6[:]))
         nc.vector.tensor_copy(vsg[:], vss[:].indirect(o6[:]))
 
-        gp, gb = new("gp", PACK * O, F32), new("gb", PACK * O, F32)
-        for t in range(PACK):
-            cols = slice(t * O, (t + 1) * O)
-            nc.scalar.activation(out=gb[:, cols], in_=b[t][:].indirect(o5[:]), func=COPY, scale=a[t][:, 0:1])
-            nc.scalar.activation(out=gp[:, cols], in_=pw[t][:].indirect(o4[:]), func=COPY, scale=b[t][:, 0:1])
-
         hid = new("hid", O * PACK, BF16)
-        by_slot = "p (t c i) -> p c t i"
-        nc.vector.tensor_tensor(
-            out=hid[:].rearrange("p (c i t) -> p c t i", i=4, t=PACK),
-            in0=gp[:].rearrange(by_slot, t=PACK, i=4),
-            in1=gb[:].rearrange(by_slot, t=PACK, i=4),
-            op=MAX,
-        )
+        for t in range(PACK):
+            gp, gb = new("gp%d" % t, O, F32), new("gb%d" % t, O, F32)
+            nc.scalar.activation(out=gb[:], in_=b[t][:].indirect(o5[:]), func=COPY, scale=a[t][:, 0:1])
+            nc.scalar.activation(out=gp[:], in_=pw[t][:].indirect(o4[:]), func=COPY, scale=b[t][:, 0:1])
+            nc.vector.tensor_tensor(out=hid[:].rearrange("p (o t) -> p t o", t=PACK)[:, t, :], in0=gp[:], in1=gb[:], op=MAX)
         hw, hs = new("hw", O, U32), new("hs", O, U8)
         nc.vector.quantize_mx(out=hw[:].bitcast(E5M2), scales=hs[:], in_=hid[:])
 

@@ -46,7 +46,7 @@ def tile_list_ownlead_storeleads_store_plain_kernel(tc, xt_words, xt_scales, wt_
             for q in range(4):
                 engs[q].dma_start(out=tile[32 * q : 32 * q + 32, :].bitcast(I32), in_=src[0, 4 * q : 4 * q + 4, :].bitcast(I32).partition_broadcast(8))
 
-        xs, ws, w2s, vss = shared.tile([P, T], U8, name="xs", align_bytes=64, offset=0), new("ws", V, U8), new("w2s", R, U8), new("vss", S, U8)
+        xs, ws, w2s, vss = shared.tile([P, T], U8, name="xs", align_bytes=64, offset=0), new("ws", V, U8), new("w2s", R, U8), shared.tile([P, S], U8, name="vss", align_bytes=64, offset=3200)
         xw, ww, w2w, vsw = new("xw", T, U16), new("ww", V, U32), new("w2w", R, U32), new("vsw", S, U32)
         for tile in (w2s, vss):
             nc.vector.memset(tile[:].bitcast(I32), 0)
@@ -116,7 +116,7 @@ def tile_list_ownlead_storeleads_store_plain_kernel(tc, xt_words, xt_scales, wt_
         nc.vector.tensor_copy(vwg[:], vsw[:].indirect(o6[:]))
         nc.vector.tensor_copy(vsg[:], vss[:].indirect(o6[:]))
 
-        hid = new("hid", O * PACK, BF16)
+        hid = shared.tile([P, O * PACK], BF16, name="hid", align_bytes=64, offset=3200)
         for t in range(PACK):
             gp, gb = new("gp%d" % t, O, F32), new("gb%d" % t, O, F32)
             nc.scalar.activation(out=gb[:], in_=b[t][:].indirect(o5[:]), func=COPY, scale=a[t][:, 0:1])

from contextlib import ExitStack

import concourse.mybir as mybir

F32 = mybir.dt.float32
BF16 = mybir.dt.bfloat16
I32 = mybir.dt.int32
U32 = mybir.dt.uint32
U16 = mybir.dt.uint16
U8 = mybir.dt.uint8
E4M3 = mybir.dt.float8_e4m3fn_x4
E5M2 = mybir.dt.float8_e5m2_x4
E2M1 = mybir.dt.float4_e2m1fn_x4
COPY = mybir.ActivationFunctionType.Copy
MAX = mybir.AluOpType.max

K, T, J, R, V, C, O, N, S = 512, 1024, 256, 512, 1024, 512, 128, 256, 1024
P = 128
PACK = 4
FLOPS = 2 * K * R * J * 2 + 2 * R * N * O


def tile_list_ownlead_storeleads_store_plain_kernel(tc, xt_words, xt_scales, wt_words, wt_scales, w2_words, w2_scales, vs_words, vs_scales, offs, offs2, offs3, offs4, offs5, offs6, out):
    nc = tc.nc
    with ExitStack() as ctx:
        sb = ctx.enter_context(tc.tile_pool(name="sb", bufs=1))
        shared = ctx.enter_context(tc.tile_pool(name="shared", bufs=1))
        ps = ctx.enter_context(tc.psum_pool(name="ps", bufs=1))

        def new(name, cols, dtype):
            return sb.tile([P, cols], dtype, name=name, align_bytes=64)

        def load_list(name, src):
            tile = sb.tile(list(src.shape), U16, name=name)
            nc.sync.dma_start(tile[:], src)
            return tile

        def load_words(eng, tile, src):
            eng.dma_start(out=tile[:].bitcast(I32), in_=src.bitcast(I32))

        def load_scales(eng, tile, src):
            for q in range(4):
                eng.dma_start(out=tile[32 * q : 32 * q + 4, :].bitcast(I32), in_=src[0, 4 * q : 4 * q + 4, :].bitcast(I32))

        def load_scales_whole(engs, tile, src):
            for q in range(4):
                engs[q].dma_start(out=tile[32 * q : 32 * q + 32, :].bitcast(I32), in_=src[0, 4 * q : 4 * q + 4, :].bitcast(I32).partition_broadcast(8))

        xs, ws, w2s, vss = shared.tile([P, T], U8, name="xs", align_bytes=64, offset=0), new("ws", V, U8), new("w2s", R, U8), shared.tile([P, S], U8, name="vss", align_bytes=64, offset=3200)
        xw, ww, w2w, vsw = new("xw", T, U16), new("ww", V, U32), new("w2w", R, U32), new("vsw", S, U32)
        for tile in (w2s, vss):
            nc.vector.memset(tile[:].bitcast(I32), 0)
        pw = [new("pw%d" % t, C, F32) for t in range(PACK)]
        for t in range(PACK):
            nc.vector.memset(pw[t][:], 0.0)

        merge = "p n t -> p (n t)"
        o1 = load_list("o1", offs)
        load_scales_whole([nc.scalar, nc.sync, nc.scalar, nc.sync], ws, wt_scales)
        o2 = load_list("o2", offs2)
        load_words(nc.scalar, xw, xt_words[0])
        load_words(nc.sync, ww, wt_words[0].rearrange(merge))
        o3 = load_list("o3", offs3)
        load_scales_whole([nc.sync] * 4, xs, xt_scales)
        load_words(nc.sync, w2w, w2_words[0].rearrange(merge))
        load_scales(nc.sync, w2s, w2_scales)
        o4 = load_list("o4", offs4)
        o5 = load_list("o5", offs5)
        o6 = load_list("o6", offs6)
        load_words(nc.sync, vsw, vs_words[0].rearrange(merge))
        load_scales(nc.sync, vss, vs_scales)

        xwg, xsg = new("xwg", J, U16), new("xsg", J, U8)
        wwg, wsg = new("wwg", R, U32), new("wsg", R, U8)
        nc.vector.tensor_copy(wsg[:], ws[:].indirect(o1[:]))
        nc.vector.tensor_copy(xwg[:], xw[:].indirect(o2[:]))
        nc.vector.tensor_copy(wwg[:], ww[:].indirect(o1[:]))

        def deal(dst, src, lo, hi):
            nc.vector.tensor_copy(dst.rearrange("p (t m) -> p m t", t=hi - lo), src.rearrange("p (m t) -> p m t", t=PACK)[:, :, lo:hi])

        ww0, ws0 = new("ww0", P, U32), new("ws0", P, U8)
        ww3, ws3 = shared.tile([P, 3 * P], U32, name="ww3", align_bytes=64, offset=640), shared.tile([P, 3 * P], U8, name="ws3", align_bytes=64, offset=256)
        deal(ws0[:], wsg[:], 0, 1)
        deal(ww0[:].bitcast(I32), wwg[:].bitcast(I32), 0, 1)
        nc.vector.tensor_copy(xsg[:], xs[:].indirect(o2[:]))
        a_ps = [ps.tile([P, J], F32, name="a_ps%d" % t) for t in range(PACK)]
        b_ps = [ps.tile([P, 2, J], F32, name="b_ps%d" % h) for h in range(2)]
        a = [new("a%d" % t, J, F32) for t in range(PACK)]
        b = [new("b%d" % t, J, F32) for t in range(PACK)]

        def first_product(dst, words, scales, fmt):
            nc.tensor.matmul_mx(out=dst, lhsT=words.bitcast(fmt), lhsT_scale=scales, rhs=xwg[:].bitcast(E2M1), rhs_scale=xsg[:], start=True, stop=True)

        first_product(a_ps[0][:], ww0[:], ws0[:], E5M2)
        nc.scalar.copy(a[0][:], a_ps[0][:])
        nc.scalar.activation(out=pw[0][:].indirect(o3[:]), in_=a[0][:], func=COPY)
        deal(ws3[:], wsg[:], 1, PACK)
        deal(ww3[:].bitcast(I32), wwg[:].bitcast(I32), 1, PACK)
        for t in range(1, PACK):
            cols = slice((t - 1) * P, t * P)
            first_product(a_ps[t][:], ww3[:, cols], ws3[:, cols], E5M2)
            nc.vector.tensor_copy(a[t][:], a_ps[t][:])
            nc.scalar.activation(out=pw[t][:].indirect(o3[:]), in_=a[t][:], func=COPY)

        w2wd, w2sd = shared.tile([P, R], U32, name="w2wd", align_bytes=64, offset=1152), shared.tile([P, R], U8, name="w2sd", align_bytes=64, offset=640)
        deal(w2sd[:], w2s[:], 0, PACK)
        deal(w2wd[:].bitcast(I32), w2w[:].bitcast(I32), 0, PACK)
        for t in range(PACK):
            cols = slice(t * P, (t + 1) * P)
            first_product(b_ps[t // 2][:, t % 2, :], w2wd[:, cols], w2sd[:, cols], E4M3)
        for t in range(PACK):
            nc.vector.tensor_copy(b[t][:], b_ps[t // 2][:, t % 2, :])

        vwg, vsg = shared.tile([P, N], U32, name="vwg", align_bytes=64, offset=1408), shared.tile([P, N], U8, name="vsg", align_bytes=64, offset=1152)
        nc.vector.tensor_copy(vwg[:], vsw[:].indirect(o6[:]))
        nc.vector.tensor_copy(vsg[:], vss[:].indirect(o6[:]))

        hid = shared.tile([P, O * PACK], BF16, name="hid", align_bytes=64, offset=3200)
        for t in range(PACK):
            gp, gb = new("gp%d" % t, O, F32), new("gb%d" % t, O, F32)
            nc.scalar.activation(out=gb[:], in_=b[t][:].indirect(o5[:]), func=COPY, scale=a[t][:, 0:1])
            nc.scalar.activation(out=gp[:], in_=pw[t][:].indirect(o4[:]), func=COPY, scale=b[t][:, 0:1])
            nc.vector.tensor_tensor(out=hid[:].rearrange("p (o t) -> p t o", t=PACK)[:, t, :], in0=gp[:], in1=gb[:], op=MAX)
        hw, hs = new("hw", O, U32), new("hs", O, U8)
        nc.vector.quantize_mx(out=hw[:].bitcast(E5M2), scales=hs[:], in_=hid[:])

        for h in range(2):
            cols = slice(h * P, (h + 1) * P)
            y_ps = ps.tile([P, O], F32, name="y_ps%d" % h)
            y = new("y%d" % h, O, F32)
            nc.tensor.matmul_mx(out=y_ps[:], lhsT=vwg[:, cols].bitcast(E4M3), lhsT_scale=vsg[:, cols], rhs=hw[:].bitcast(E5M2), rhs_scale=hs[:], start=True, stop=True)
            if h == 0:
                nc.vector.tensor_copy(y[:], y_ps[:])
                nc.sync.dma_start(out=out[cols, :], in_=y[:])
            else:
                nc.scalar.copy(y[:], y_ps[:])
                nc.scalar.dma_start(out=out[cols, :], in_=y[:])
